import numpy as np
import ml_dtypes


def mxq(x, axis, fmt="e4m3"):
    dtype, down = {"e4m3": (ml_dtypes.float8_e4m3fn, 7), "e5m2": (ml_dtypes.float8_e5m2, 14)}[fmt]
    v = np.moveaxis(np.asarray(x, np.float32).astype(ml_dtypes.bfloat16).astype(np.float64), axis, -1)
    blocks = v.reshape(v.shape[:-1] + (-1, 32))
    amax = np.abs(blocks).max(-1, keepdims=True)
    byte = np.maximum(np.where(amax > 0, np.frexp(amax)[1] - 1 + 127, 0) - down, 1)
    scale = np.exp2(byte - 127.0)
    codes = (blocks / scale).astype(np.float32).astype(dtype).astype(np.float64)
    return np.moveaxis((codes * scale).reshape(v.shape), -1, axis)


WIDE = False


def mx_kscale(k):
    if not WIDE:
        return np.ones(k)
    levels = np.array([10, -10, 5, -5, 0])
    if k % 512:
        return np.exp2(np.random.permutation(np.resize(levels, k // 32))).repeat(32)
    a = np.empty((k // 512, 16))
    for p in range(k // 512):
        a[p, :8] = np.random.permutation(np.resize(levels, 8))
        for g in range(8):
            far = levels[np.abs(levels - a[p, g]) >= 10]
            a[p, g + 8] = far[np.random.randint(len(far))]
    return np.exp2(a.ravel()).repeat(32)


def f64(x):
    return np.asarray(x).astype(np.float64)


def striped(idx):
    return np.tile(idx.reshape(-1, 16).T, (8, 1)).astype(np.uint16)


def unstriped(offs):
    return offs[:16].T.reshape(-1).astype(np.int64)


def gelu(v):
    return 0.5 * v * (1.0 + np.tanh(np.sqrt(2.0 / np.pi) * (v + 0.044715 * v**3)))


K, T, E, C, H, N = 512, 2048, 8, 128, 512, 256


def by_expert(wq, xq):
    return np.concatenate([wq[e].T @ xq[:, e * C:(e + 1) * C] for e in range(E)], axis=1)


def setup_inputs():
    n = np.random.standard_normal
    s = mx_kscale(K)[:, None]
    u = mx_kscale(H)
    return {
        "xT": (n((K, T)) * s).astype(np.float32),
        "w1": (n((E, K, H)) / np.sqrt(K) / s[None]).astype(np.float32),
        "w3": (n((E, K, H)) / np.sqrt(K) / s[None] * u[None, None, :]).astype(np.float32),
        "w2": (n((E, H, N)) / np.sqrt(H) / u[None, :, None]).astype(np.float32),
        "gate": np.tile(np.random.uniform(0.2, 1.0, E * C), (N, 1)).astype(np.float32),
        "offs": striped(np.random.permutation(T)[:E * C]),
    }


def reference(xT, w1, w3, w2, gate, offs):
    idx = unstriped(offs)
    xq = mxq(f64(xT)[:, idx], 0, "e4m3")
    h = gelu(by_expert(mxq(f64(w1), 1, "e4m3"), xq))
    h = h * by_expert(mxq(f64(w3), 1, "e4m3"), xq)
    y = by_expert(mxq(f64(w2), 1, "e4m3"), mxq(h, 0, "e4m3"))
    out = np.zeros((N, T))
    out[:, idx] = f64(gate) * y
    return out

@@ -1,0 +1,244 @@
+from contextlib import ExitStack
+
+import concourse.mybir as mybir
+
+K, T, E, C, H, N = 512, 2048, 8, 128, 512, 256
+FLOPS = 2 * E * C * (2 * K * H + H * N)
+
+F32 = mybir.dt.float32
+BF16 = mybir.dt.bfloat16
+U32 = mybir.dt.uint32
+U16 = mybir.dt.uint16
+U8 = mybir.dt.uint8
+FP8X4 = mybir.dt.float8_e4m3fn_x4
+MULT = mybir.AluOpType.mult
+ADD = mybir.AluOpType.add
+GELU = mybir.ActivationFunctionType.Gelu_apprx_tanh
+
+P = 128
+S = E * C
+HALF = 512
+PAIR = 2 * C
+
+SCAT = "tt"
+CAST = "SSSV"
+I1 = [[["S",0,128]],[["S",0,128]],[["S",0,128]],[["S",0,128]],[["S",0,128]],[["S",0,128]],[["S",0,128]],[["S",0,128]]]
+I3 = [[["V",0,128]],[["S",0,128]],[["V",0,128]],[["S",0,128]],[["V",0,128]],[["S",0,128]],[["S",0,128]],[["V",0,128]]]
+I2 = [[["V",0,256]],[["V",0,256]],[["V",0,256]],[["V",0,256]],[["V",0,256]],[["V",0,256]],[["S",0,256]],[["S",0,256]]]
+SC_AFTER = [3,5,7,7]
+TAIL = 6
+MS = "V"
+BUFS = {"raw":10,"raw2":4,"grp":4,"grp2":2,"cod":3,"cod2":4,"act":3}
+
+
+def tile_routed_moe_kernel(tc, xT, w1, w3, w2, gate, offs, out):
+    nc = tc.nc
+
+    def copy_on(eng, dst, src):
+        if eng == "S":
+            nc.scalar.copy(out=dst, in_=src)
+        elif eng == "V":
+            nc.vector.tensor_copy(out=dst, in_=src)
+        else:
+            nc.gpsimd.tensor_scalar(out=dst, in0=src, scalar1=1.0, scalar2=0.0, op0=MULT, op1=ADD)
+
+    with ExitStack() as ctx:
+        lists = ctx.enter_context(tc.tile_pool(name="lists", bufs=1))
+        keep = ctx.enter_context(tc.tile_pool(name="keep", bufs=1))
+        raw = ctx.enter_context(tc.tile_pool(name="raw", bufs=BUFS["raw"]))
+        raw2 = ctx.enter_context(tc.tile_pool(name="raw2", bufs=BUFS["raw2"]))
+        grp = ctx.enter_context(tc.tile_pool(name="grp", bufs=BUFS["grp"]))
+        grp2 = ctx.enter_context(tc.tile_pool(name="grp2", bufs=BUFS["grp2"]))
+        cod = ctx.enter_context(tc.tile_pool(name="cod", bufs=BUFS["cod"]))
+        cod2 = ctx.enter_context(tc.tile_pool(name="cod2", bufs=BUFS["cod2"]))
+        act = ctx.enter_context(tc.tile_pool(name="act", bufs=BUFS["act"]))
+        ysp = ctx.enter_context(tc.tile_pool(name="ysp", bufs=4))
+        hid = ctx.enter_context(tc.tile_pool(name="hid", bufs=2))
+        ps_a = ctx.enter_context(tc.psum_pool(name="ps_a", bufs=3))
+        ps_b = ctx.enter_context(tc.psum_pool(name="ps_b", bufs=3))
+        ps_y = ctx.enter_context(tc.psum_pool(name="ps_y", bufs=2))
+
+        offs_sb = lists.tile([P, S // 16], U16, name="offs_sb")
+        nc.sync.dma_start(offs_sb[:], offs)
+
+        warm = keep.tile([P, 1], F32, name="warm")
+        nc.vector.memset(warm[:], 0.0)
+        nc.scalar.activation(out=warm[:], in_=warm[:], func=GELU)
+
+        win = [keep.tile([P, T], F32, name="win%d" % nt) for nt in range(2)]
+        for nt in range(2):
+            if MS == "G":
+                nc.gpsimd.memset(win[nt][:], 0.0)
+            else:
+                nc.vector.memset(win[nt][:], 0.0)
+
+        xv = xT.rearrange("(p t) n -> p t n", t=4)
+        pair = [keep.tile([P, 2 * T], BF16, name="pair%d" % u) for u in range(2)]
+        xg = [keep.tile([P, 4 * HALF], BF16, name="xg%d" % s, align_bytes=64) for s in range(2)]
+        xc = keep.tile([P, S], U32, name="xc", align_bytes=64)
+        xs = keep.tile([P, S], U8, name="xs", align_bytes=64)
+        TH = T // 2
+        rx = {}
+        for u in range(2):
+            for h in range(2):
+                rx[(u, h)] = raw.tile([P, 2, TH], F32, name="rw")
+                nc.sync.dma_start(rx[(u, h)][:], xv[:, 2 * u : 2 * u + 2, h * TH : (h + 1) * TH])
+        for u in range(2):
+            for h in range(2):
+                copy_on(
+                    CAST[2 * u + h],
+                    pair[u][:, h * 2 * TH : (h + 1) * 2 * TH].rearrange("p (n j) -> p n j", j=2),
+                    rx[(u, h)][:].rearrange("p j n -> p n j"),
+                )
+            for s in range(2):
+                nc.vector.tensor_copy(
+                    out=xg[s][:].bitcast(U32).rearrange("p (n u) -> p n u", u=2)[:, :, u],
+                    in_=pair[u][:].bitcast(U32).indirect(offs_sb[:, s * (HALF // 16) : (s + 1) * (HALF // 16)]),
+                )
+        for s in range(2):
+            nc.vector.quantize_mx(
+                out=xc[:, s * HALF : (s + 1) * HALF].bitcast(FP8X4),
+                scales=xs[:, s * HALF : (s + 1) * HALF],
+                in_=xg[s][:],
+            )
+
+        w1v = w1.rearrange("e (p j) c -> e p j c", j=4)
+        w3v = w3.rearrange("e (p j) c -> e p j c", j=4)
+        w2v = w2.rearrange("e (p j) c -> e p j c", j=4)
+        gv = gate.rearrange("(nt p) s -> p nt s", p=P)
+
+        gate_sb = {}
+        wc2 = {}
+        ws2 = {}
+        ysb = {}
+        state = {}
+
+        def load_gate(q):
+            gate_sb[q] = keep.tile([P, 2, PAIR], F32, name="gate%d" % q)
+            nc.sync.dma_start(gate_sb[q][:], gv[:, :, q * PAIR : (q + 1) * PAIR])
+
+        def load_w2(e):
+            r2 = raw2.tile([P, 4, N], F32, name="rw2")
+            nc.sync.dma_start(r2[:], w2v[e])
+            return r2
+
+        def prep_w2(e, r2):
+            g2 = grp2.tile([P, 4 * N], BF16, name="g2", align_bytes=64)
+            for eng, c0, c1 in I2[e]:
+                if eng == "G":
+                    copy_on(
+                        eng,
+                        g2[:, 4 * c0 : 4 * c1].rearrange("p (c j) -> p c j", j=4),
+                        r2[:, :, c0:c1].rearrange("p j c -> p c j"),
+                    )
+                else:
+                    copy_on(
+                        eng,
+                        g2[:, 4 * c0 : 4 * c1].rearrange("p (c i j) -> p c j i", i=4, j=4),
+                        r2[:, :, c0:c1].rearrange("p j (c i) -> p c j i", i=4),
+                    )
+            wc2[e] = cod2.tile([P, N], U32, name="wc2", align_bytes=64)
+            ws2[e] = cod2.tile([P, N], U8, name="ws2", align_bytes=64)
+            nc.vector.quantize_mx(out=wc2[e][:].bitcast(FP8X4), scales=ws2[e][:], in_=g2[:])
+
+        def scatter(q):
+            cols = offs_sb[:, q * (PAIR // 16) : (q + 1) * (PAIR // 16)]
+            for nt in range(2):
+                if SCAT == "tt":
+                    nc.vector.tensor_tensor(
+                        out=win[nt][:].indirect(cols), in0=ysb[q][:, nt, :], in1=gate_sb[q][:, nt, :], op=MULT
+                    )
+                else:
+                    nc.vector.tensor_copy(out=win[nt][:].indirect(cols), in_=ysb[q][:, nt, :])
+
+        late_w2 = {}
+        for e in range(E):
+            el = e % 2
+            q = e // 2
+            banks = []
+            raws = []
+            for wv in (w1v, w3v):
+                r = raw.tile([P, 4, H], F32, name="rw")
+                nc.sync.dma_start(r[:], wv[e])
+                raws.append(r)
+            r2 = None
+            if e < TAIL:
+                r2 = load_w2(e)
+                if el == 1:
+                    load_gate(q)
+            if e == E - 1:
+                for ee in range(TAIL, E):
+                    late_w2[ee] = load_w2(ee)
+                for qq in range(TAIL // 2, E // 2):
+                    load_gate(qq)
+            for which, r, parts, pool in (("1", raws[0], I1[e], ps_a), ("3", raws[1], I3[e], ps_b)):
+                g = grp.tile([P, 4 * H], BF16, name="g13", align_bytes=64)
+                for eng, m0, m1 in parts:
+                    copy_on(
+                        eng,
+                        g[:].rearrange("p (t m j) -> p m j t", t=4, j=4)[:, m0:m1],
+                        r[:].rearrange("p j (m t) -> p m j t", t=4)[:, m0:m1],
+                    )
+                wc = cod.tile([P, H], U32, name="wc" + which, align_bytes=64)
+                ws = cod.tile([P, H], U8, name="ws" + which, align_bytes=64)
+                nc.vector.quantize_mx(out=wc[:].bitcast(FP8X4), scales=ws[:], in_=g[:])
+                bank = pool.tile([P, 4, C], F32, name="bank" + which)
+                for t in range(4):
+                    nc.tensor.matmul_mx(
+                        out=bank[:, t, :],
+                        lhsT=wc[:, t * P : (t + 1) * P].bitcast(FP8X4),
+                        lhsT_scale=ws[:, t * P : (t + 1) * P],
+                        rhs=xc[:, e * C : (e + 1) * C].bitcast(FP8X4),
+                        rhs_scale=xs[:, e * C : (e + 1) * C],
+                        start=True,
+                        stop=True,
+                    )
+                banks.append(bank)
+
+            gl = act.tile([P, 4 * C], F32, name="gl")
+            nc.scalar.activation(
+                out=gl[:].rearrange("p (n t) -> p n t", t=4),
+                in_=banks[0][:].rearrange("p t n -> p n t"),
+                func=GELU,
+            )
+            if el == 0:
+                state["hb"] = hid.tile([P, 4 * PAIR], BF16, name="hb", align_bytes=64)
+            hb = state["hb"]
+            nc.vector.tensor_tensor(
+                out=hb[:, el * 4 * C : (el + 1) * 4 * C].rearrange("p (n t) -> p n t", t=4),
+                in0=gl[:].rearrange("p (n t) -> p n t", t=4),
+                in1=banks[1][:].rearrange("p t n -> p n t"),
+                op=MULT,
+            )
+            if r2 is not None:
+                prep_w2(e, r2)
+            if e == E - 1:
+                for ee in range(TAIL, E):
+                    prep_w2(ee, late_w2[ee])
+            if el == 1:
+                hc = hid.tile([P, PAIR], U32, name="hc", align_bytes=64)
+                hs = hid.tile([P, PAIR], U8, name="hs", align_bytes=64)
+                nc.vector.quantize_mx(out=hc[:].bitcast(FP8X4), scales=hs[:], in_=hb[:])
+                py = ps_y.tile([P, 2, PAIR], F32, name="py")
+                for nt in range(2):
+                    for l in range(2):
+                        ee = 2 * q + l
+                        nc.tensor.matmul_mx(
+                            out=py[:, nt, l * C : (l + 1) * C],
+                            lhsT=wc2[ee][:, nt * P : (nt + 1) * P].bitcast(FP8X4),
+                            lhsT_scale=ws2[ee][:, nt * P : (nt + 1) * P],
+                            rhs=hc[:, l * C : (l + 1) * C].bitcast(FP8X4),
+                            rhs_scale=hs[:, l * C : (l + 1) * C],
+                            start=True,
+                            stop=True,
+                        )
+                ysb[q] = ysp.tile([P, 2, PAIR], F32, name="ysb")
+                if SCAT == "tt":
+                    nc.scalar.copy(out=ysb[q][:], in_=py[:])
+                else:
+                    nc.vector.tensor_tensor(out=ysb[q][:], in0=py[:], in1=gate_sb[q][:], op=MULT)
+            for qq in range(E // 2):
+                if SC_AFTER[qq] == e:
+                    scatter(qq)
+        for nt in range(2):
+            nc.sync.dma_start(out[nt * P : (nt + 1) * P, :], win[nt][:])

@@ -28,6 +28,8 @@ I2 = [[["V",0,256]],[["V",0,256]],[["V",0,256]],[["V",0,256]],[["V",0,256]],[["V
 SC_AFTER = [3,5,7,7]
 TAIL = 6
 MS = "V"
+YSPLIT = [3]
+QH1 = [3]
 BUFS = {"raw":10,"raw2":4,"grp":4,"grp2":2,"cod":3,"cod2":4,"act":3}
 
 
@@ -215,16 +217,37 @@ def tile_routed_moe_kernel(tc, xT, w1, w3, w2, gate, offs, out):
             if e == E - 1:
                 for ee in range(TAIL, E):
                     prep_w2(ee, late_w2[ee])
+            if q in QH1:
+                if el == 0:
+                    state["hc"] = hid.tile([P, PAIR], U32, name="hc", align_bytes=64)
+                    state["hs"] = hid.tile([P, PAIR], U8, name="hs", align_bytes=64)
+                nc.vector.quantize_mx(
+                    out=state["hc"][:, el * C : (el + 1) * C].bitcast(FP8X4),
+                    scales=state["hs"][:, el * C : (el + 1) * C],
+                    in_=hb[:, el * 4 * C : (el + 1) * 4 * C],
+                )
             if el == 1:
-                hc = hid.tile([P, PAIR], U32, name="hc", align_bytes=64)
-                hs = hid.tile([P, PAIR], U8, name="hs", align_bytes=64)
-                nc.vector.quantize_mx(out=hc[:].bitcast(FP8X4), scales=hs[:], in_=hb[:])
-                py = ps_y.tile([P, 2, PAIR], F32, name="py")
+                if q in QH1:
+                    hc = state["hc"]
+                    hs = state["hs"]
+                else:
+                    hc = hid.tile([P, PAIR], U32, name="hc", align_bytes=64)
+                    hs = hid.tile([P, PAIR], U8, name="hs", align_bytes=64)
+                    nc.vector.quantize_mx(out=hc[:].bitcast(FP8X4), scales=hs[:], in_=hb[:])
+                ysb[q] = ysp.tile([P, 2, PAIR], F32, name="ysb")
+                if q in YSPLIT:
+                    pys = []
+                    for nt in range(2):
+                        py = ps_y.tile([P, PAIR], F32, name="py")
+                        pys.append(py[:])
+                else:
+                    py = ps_y.tile([P, 2, PAIR], F32, name="py")
+                    pys = [py[:, 0, :], py[:, 1, :]]
                 for nt in range(2):
                     for l in range(2):
                         ee = 2 * q + l
                         nc.tensor.matmul_mx(
-                            out=py[:, nt, l * C : (l + 1) * C],
+                            out=pys[nt][:, l * C : (l + 1) * C],
                             lhsT=wc2[ee][:, nt * P : (nt + 1) * P].bitcast(FP8X4),
                             lhsT_scale=ws2[ee][:, nt * P : (nt + 1) * P],
                             rhs=hc[:, l * C : (l + 1) * C].bitcast(FP8X4),
@@ -232,11 +255,10 @@ def tile_routed_moe_kernel(tc, xT, w1, w3, w2, gate, offs, out):
                             start=True,
                             stop=True,
                         )
-                ysb[q] = ysp.tile([P, 2, PAIR], F32, name="ysb")
-                if SCAT == "tt":
+                    if q in YSPLIT:
+                        nc.scalar.copy(out=ysb[q][:, nt, :], in_=pys[nt])
+                if q not in YSPLIT:
                     nc.scalar.copy(out=ysb[q][:], in_=py[:])
-                else:
-                    nc.vector.tensor_tensor(out=ysb[q][:], in0=py[:], in1=gate_sb[q][:], op=MULT)
             for qq in range(E // 2):
                 if SC_AFTER[qq] == e:
                     scatter(qq)

@@ -12,7 +12,6 @@ U16 = mybir.dt.uint16
 U8 = mybir.dt.uint8
 FP8X4 = mybir.dt.float8_e4m3fn_x4
 MULT = mybir.AluOpType.mult
-ADD = mybir.AluOpType.add
 GELU = mybir.ActivationFunctionType.Gelu_apprx_tanh
 
 P = 128
@@ -20,17 +19,13 @@ S = E * C
 HALF = 512
 PAIR = 2 * C
 
-SCAT = "tt"
-CAST = "SSSV"
-I1 = [[["S",0,128]],[["S",0,128]],[["S",0,128]],[["S",0,128]],[["S",0,128]],[["S",0,128]],[["S",0,128]],[["S",0,128]]]
-I3 = [[["V",0,128]],[["S",0,128]],[["V",0,128]],[["S",0,128]],[["V",0,128]],[["S",0,128]],[["S",0,128]],[["V",0,128]]]
-I2 = [[["V",0,256]],[["V",0,256]],[["V",0,256]],[["V",0,256]],[["V",0,256]],[["V",0,256]],[["S",0,256]],[["S",0,256]]]
-SC_AFTER = [3,5,7,7]
-TAIL = 6
-MS = "V"
-YSPLIT = [3]
-QH1 = [3]
-BUFS = {"raw":10,"raw2":4,"grp":4,"grp2":2,"cod":3,"cod2":4,"act":3}
+XCUT = 768
+I1 = [[["S", 0, 128]]] * E
+I3 = [[["V", 0, 128]], [["S", 0, 128]]] * (E // 2)
+I2 = [[["V", 0, 256]]] * E
+SC_AFTER = [3, 5, 7, 7]
+LAST = E // 2 - 1
+BUFS = {"raw": 9, "rawx": 2, "raw2": 2, "grp": 4, "grp2": 2, "cod": 3, "cod2": 4, "act": 3}
 
 
 def tile_routed_moe_kernel(tc, xT, w1, w3, w2, gate, offs, out):
@@ -39,15 +34,14 @@ def tile_routed_moe_kernel(tc, xT, w1, w3, w2, gate, offs, out):
     def copy_on(eng, dst, src):
         if eng == "S":
             nc.scalar.copy(out=dst, in_=src)
-        elif eng == "V":
-            nc.vector.tensor_copy(out=dst, in_=src)
         else:
-            nc.gpsimd.tensor_scalar(out=dst, in0=src, scalar1=1.0, scalar2=0.0, op0=MULT, op1=ADD)
+            nc.vector.tensor_copy(out=dst, in_=src)
 
     with ExitStack() as ctx:
         lists = ctx.enter_context(tc.tile_pool(name="lists", bufs=1))
         keep = ctx.enter_context(tc.tile_pool(name="keep", bufs=1))
         raw = ctx.enter_context(tc.tile_pool(name="raw", bufs=BUFS["raw"]))
+        rawx = ctx.enter_context(tc.tile_pool(name="rawx", bufs=BUFS["rawx"]))
         raw2 = ctx.enter_context(tc.tile_pool(name="raw2", bufs=BUFS["raw2"]))
         grp = ctx.enter_context(tc.tile_pool(name="grp", bufs=BUFS["grp"]))
         grp2 = ctx.enter_context(tc.tile_pool(name="grp2", bufs=BUFS["grp2"]))
@@ -69,28 +63,23 @@ def tile_routed_moe_kernel(tc, xT, w1, w3, w2, gate, offs, out):
 
         win = [keep.tile([P, T], F32, name="win%d" % nt) for nt in range(2)]
         for nt in range(2):
-            if MS == "G":
-                nc.gpsimd.memset(win[nt][:], 0.0)
-            else:
-                nc.vector.memset(win[nt][:], 0.0)
+            nc.vector.memset(win[nt][:], 0.0)
 
         xv = xT.rearrange("(p t) n -> p t n", t=4)
         pair = [keep.tile([P, 2 * T], BF16, name="pair%d" % u) for u in range(2)]
         xg = [keep.tile([P, 4 * HALF], BF16, name="xg%d" % s, align_bytes=64) for s in range(2)]
         xc = keep.tile([P, S], U32, name="xc", align_bytes=64)
         xs = keep.tile([P, S], U8, name="xs", align_bytes=64)
-        TH = T // 2
-        rx = {}
+        rx = []
         for u in range(2):
-            for h in range(2):
-                rx[(u, h)] = raw.tile([P, 2, TH], F32, name="rw")
-                nc.sync.dma_start(rx[(u, h)][:], xv[:, 2 * u : 2 * u + 2, h * TH : (h + 1) * TH])
+            rx.append(rawx.tile([P, 2, T], F32, name="rwx"))
+            nc.sync.dma_start(rx[u][:], xv[:, 2 * u : 2 * u + 2, :])
         for u in range(2):
-            for h in range(2):
+            for eng, n0, n1 in (("S", 0, XCUT), ("V", XCUT, T)):
                 copy_on(
-                    CAST[2 * u + h],
-                    pair[u][:, h * 2 * TH : (h + 1) * 2 * TH].rearrange("p (n j) -> p n j", j=2),
-                    rx[(u, h)][:].rearrange("p j n -> p n j"),
+                    eng,
+                    pair[u][:, 2 * n0 : 2 * n1].rearrange("p (n j) -> p n j", j=2),
+                    rx[u][:, :, n0:n1].rearrange("p j n -> p n j"),
                 )
             for s in range(2):
                 nc.vector.tensor_copy(
@@ -106,7 +95,7 @@ def tile_routed_moe_kernel(tc, xT, w1, w3, w2, gate, offs, out):
 
         w1v = w1.rearrange("e (p j) c -> e p j c", j=4)
         w3v = w3.rearrange("e (p j) c -> e p j c", j=4)
-        w2v = w2.rearrange("e (p j) c -> e p j c", j=4)
+        w2v = w2.rearrange("(q e) (p j) c -> q p e (j c)", e=2, j=4)
         gv = gate.rearrange("(nt p) s -> p nt s", p=P)
 
         gate_sb = {}
@@ -119,26 +108,14 @@ def tile_routed_moe_kernel(tc, xT, w1, w3, w2, gate, offs, out):
             gate_sb[q] = keep.tile([P, 2, PAIR], F32, name="gate%d" % q)
             nc.sync.dma_start(gate_sb[q][:], gv[:, :, q * PAIR : (q + 1) * PAIR])
 
-        def load_w2(e):
-            r2 = raw2.tile([P, 4, N], F32, name="rw2")
-            nc.sync.dma_start(r2[:], w2v[e])
-            return r2
-
         def prep_w2(e, r2):
             g2 = grp2.tile([P, 4 * N], BF16, name="g2", align_bytes=64)
             for eng, c0, c1 in I2[e]:
-                if eng == "G":
-                    copy_on(
-                        eng,
-                        g2[:, 4 * c0 : 4 * c1].rearrange("p (c j) -> p c j", j=4),
-                        r2[:, :, c0:c1].rearrange("p j c -> p c j"),
-                    )
-                else:
-                    copy_on(
-                        eng,
-                        g2[:, 4 * c0 : 4 * c1].rearrange("p (c i j) -> p c j i", i=4, j=4),
-                        r2[:, :, c0:c1].rearrange("p j (c i) -> p c j i", i=4),
-                    )
+                copy_on(
+                    eng,
+                    g2[:, 4 * c0 : 4 * c1].rearrange("p (c i j) -> p c j i", i=4, j=4),
+                    r2.rearrange("p (j c) -> p j c", j=4)[:, :, c0:c1].rearrange("p j (c i) -> p c j i", i=4),
+                )
             wc2[e] = cod2.tile([P, N], U32, name="wc2", align_bytes=64)
             ws2[e] = cod2.tile([P, N], U8, name="ws2", align_bytes=64)
             nc.vector.quantize_mx(out=wc2[e][:].bitcast(FP8X4), scales=ws2[e][:], in_=g2[:])
@@ -146,14 +123,10 @@ def tile_routed_moe_kernel(tc, xT, w1, w3, w2, gate, offs, out):
         def scatter(q):
             cols = offs_sb[:, q * (PAIR // 16) : (q + 1) * (PAIR // 16)]
             for nt in range(2):
-                if SCAT == "tt":
-                    nc.vector.tensor_tensor(
-                        out=win[nt][:].indirect(cols), in0=ysb[q][:, nt, :], in1=gate_sb[q][:, nt, :], op=MULT
-                    )
-                else:
-                    nc.vector.tensor_copy(out=win[nt][:].indirect(cols), in_=ysb[q][:, nt, :])
+                nc.vector.tensor_tensor(
+                    out=win[nt][:].indirect(cols), in0=ysb[q][:, nt, :], in1=gate_sb[q][:, nt, :], op=MULT
+                )
 
-        late_w2 = {}
         for e in range(E):
             el = e % 2
             q = e // 2
@@ -163,16 +136,10 @@ def tile_routed_moe_kernel(tc, xT, w1, w3, w2, gate, offs, out):
                 r = raw.tile([P, 4, H], F32, name="rw")
                 nc.sync.dma_start(r[:], wv[e])
                 raws.append(r)
-            r2 = None
-            if e < TAIL:
-                r2 = load_w2(e)
-                if el == 1:
-                    load_gate(q)
-            if e == E - 1:
-                for ee in range(TAIL, E):
-                    late_w2[ee] = load_w2(ee)
-                for qq in range(TAIL // 2, E // 2):
-                    load_gate(qq)
+            if el == 1:
+                r2 = raw2.tile([P, 2, 4 * N], F32, name="rw2")
+                nc.sync.dma_start(r2[:], w2v[q])
+                load_gate(q)
             for which, r, parts, pool in (("1", raws[0], I1[e], ps_a), ("3", raws[1], I3[e], ps_b)):
                 g = grp.tile([P, 4 * H], BF16, name="g13", align_bytes=64)
                 for eng, m0, m1 in parts:
@@ -205,37 +172,31 @@ def tile_routed_moe_kernel(tc, xT, w1, w3, w2, gate, offs, out):
             )
             if el == 0:
                 state["hb"] = hid.tile([P, 4 * PAIR], BF16, name="hb", align_bytes=64)
+                state["hc"] = hid.tile([P, PAIR], U32, name="hc", align_bytes=64)
+                state["hs"] = hid.tile([P, PAIR], U8, name="hs", align_bytes=64)
             hb = state["hb"]
+            hc = state["hc"]
+            hs = state["hs"]
             nc.vector.tensor_tensor(
                 out=hb[:, el * 4 * C : (el + 1) * 4 * C].rearrange("p (n t) -> p n t", t=4),
                 in0=gl[:].rearrange("p (n t) -> p n t", t=4),
                 in1=banks[1][:].rearrange("p t n -> p n t"),
                 op=MULT,
             )
-            if r2 is not None:
-                prep_w2(e, r2)
-            if e == E - 1:
-                for ee in range(TAIL, E):
-                    prep_w2(ee, late_w2[ee])
-            if q in QH1:
-                if el == 0:
-                    state["hc"] = hid.tile([P, PAIR], U32, name="hc", align_bytes=64)
-                    state["hs"] = hid.tile([P, PAIR], U8, name="hs", align_bytes=64)
+            if el == 1:
+                for l in range(2):
+                    prep_w2(2 * q + l, r2[:, l, :])
+            if q == LAST:
                 nc.vector.quantize_mx(
-                    out=state["hc"][:, el * C : (el + 1) * C].bitcast(FP8X4),
-                    scales=state["hs"][:, el * C : (el + 1) * C],
+                    out=hc[:, el * C : (el + 1) * C].bitcast(FP8X4),
+                    scales=hs[:, el * C : (el + 1) * C],
                     in_=hb[:, el * 4 * C : (el + 1) * 4 * C],
                 )
             if el == 1:
-                if q in QH1:
-                    hc = state["hc"]
-                    hs = state["hs"]
-                else:
-                    hc = hid.tile([P, PAIR], U32, name="hc", align_bytes=64)
-                    hs = hid.tile([P, PAIR], U8, name="hs", align_bytes=64)
+                if q != LAST:
                     nc.vector.quantize_mx(out=hc[:].bitcast(FP8X4), scales=hs[:], in_=hb[:])
                 ysb[q] = ysp.tile([P, 2, PAIR], F32, name="ysb")
-                if q in YSPLIT:
+                if q == LAST:
                     pys = []
                     for nt in range(2):
                         py = ps_y.tile([P, PAIR], F32, name="py")
@@ -255,9 +216,9 @@ def tile_routed_moe_kernel(tc, xT, w1, w3, w2, gate, offs, out):
                             start=True,
                             stop=True,
                         )
-                    if q in YSPLIT:
+                    if q == LAST:
                         nc.scalar.copy(out=ysb[q][:, nt, :], in_=pys[nt])
-                if q not in YSPLIT:
+                if q != LAST:
                     nc.scalar.copy(out=ysb[q][:], in_=py[:])
             for qq in range(E // 2):
                 if SC_AFTER[qq] == e:

@@ -21,11 +21,10 @@ PAIR = 2 * C
 
 XCUT = 768
 I1 = [[["S", 0, 128]]] * E
-I3 = [[["V", 0, 128]], [["S", 0, 128]]] * (E // 2)
-I2 = [[["V", 0, 256]]] * E
+I3 = [[["V", 0, 128]] if e in (0, 1, 2, 4, 6) else [["S", 0, 128]] for e in range(E)]
 SC_AFTER = [3, 5, 7, 7]
 LAST = E // 2 - 1
-BUFS = {"raw": 9, "rawx": 2, "raw2": 2, "grp": 4, "grp2": 2, "cod": 3, "cod2": 4, "act": 3}
+BUFS = {"raw": 9, "rawx": 2, "raw2": 2, "grp": 4, "grp2": 2, "cod": 3, "cod2": 2, "act": 3}
 
 
 def tile_routed_moe_kernel(tc, xT, w1, w3, w2, gate, offs, out):
@@ -108,17 +107,15 @@ def tile_routed_moe_kernel(tc, xT, w1, w3, w2, gate, offs, out):
             gate_sb[q] = keep.tile([P, 2, PAIR], F32, name="gate%d" % q)
             nc.sync.dma_start(gate_sb[q][:], gv[:, :, q * PAIR : (q + 1) * PAIR])
 
-        def prep_w2(e, r2):
-            g2 = grp2.tile([P, 4 * N], BF16, name="g2", align_bytes=64)
-            for eng, c0, c1 in I2[e]:
-                copy_on(
-                    eng,
-                    g2[:, 4 * c0 : 4 * c1].rearrange("p (c i j) -> p c j i", i=4, j=4),
-                    r2.rearrange("p (j c) -> p j c", j=4)[:, :, c0:c1].rearrange("p j (c i) -> p c j i", i=4),
-                )
-            wc2[e] = cod2.tile([P, N], U32, name="wc2", align_bytes=64)
-            ws2[e] = cod2.tile([P, N], U8, name="ws2", align_bytes=64)
-            nc.vector.quantize_mx(out=wc2[e][:].bitcast(FP8X4), scales=ws2[e][:], in_=g2[:])
+        def prep_w2(q, r2):
+            g2 = grp2.tile([P, 8 * N], BF16, name="g2", align_bytes=64)
+            nc.vector.tensor_copy(
+                out=g2[:].rearrange("p (l c i j) -> p l c j i", l=2, i=4, j=4),
+                in_=r2[:].rearrange("p l (j c i) -> p l c j i", j=4, i=4),
+            )
+            wc2[q] = cod2.tile([P, 2 * N], U32, name="wc2", align_bytes=64)
+            ws2[q] = cod2.tile([P, 2 * N], U8, name="ws2", align_bytes=64)
+            nc.vector.quantize_mx(out=wc2[q][:].bitcast(FP8X4), scales=ws2[q][:], in_=g2[:])
 
         def scatter(q):
             cols = offs_sb[:, q * (PAIR // 16) : (q + 1) * (PAIR // 16)]
@@ -139,7 +136,10 @@ def tile_routed_moe_kernel(tc, xT, w1, w3, w2, gate, offs, out):
             if el == 1:
                 r2 = raw2.tile([P, 2, 4 * N], F32, name="rw2")
                 nc.sync.dma_start(r2[:], w2v[q])
-                load_gate(q)
+                if q == LAST:
+                    load_gate(q)
+            elif q > 0:
+                load_gate(q - 1)
             for which, r, parts, pool in (("1", raws[0], I1[e], ps_a), ("3", raws[1], I3[e], ps_b)):
                 g = grp.tile([P, 4 * H], BF16, name="g13", align_bytes=64)
                 for eng, m0, m1 in parts:
@@ -184,8 +184,7 @@ def tile_routed_moe_kernel(tc, xT, w1, w3, w2, gate, offs, out):
                 op=MULT,
             )
             if el == 1:
-                for l in range(2):
-                    prep_w2(2 * q + l, r2[:, l, :])
+                prep_w2(q, r2)
             if q == LAST:
                 nc.vector.quantize_mx(
                     out=hc[:, el * C : (el + 1) * C].bitcast(FP8X4),
@@ -206,11 +205,11 @@ def tile_routed_moe_kernel(tc, xT, w1, w3, w2, gate, offs, out):
                     pys = [py[:, 0, :], py[:, 1, :]]
                 for nt in range(2):
                     for l in range(2):
-                        ee = 2 * q + l
+                        w0 = l * N + nt * P
                         nc.tensor.matmul_mx(
                             out=pys[nt][:, l * C : (l + 1) * C],
-                            lhsT=wc2[ee][:, nt * P : (nt + 1) * P].bitcast(FP8X4),
-                            lhsT_scale=ws2[ee][:, nt * P : (nt + 1) * P],
+                            lhsT=wc2[q][:, w0 : w0 + P].bitcast(FP8X4),
+                            lhsT_scale=ws2[q][:, w0 : w0 + P],
                             rhs=hc[:, l * C : (l + 1) * C].bitcast(FP8X4),
                             rhs_scale=hs[:, l * C : (l + 1) * C],
                             start=True,

@@ -16,15 +16,15 @@ GELU = mybir.ActivationFunctionType.Gelu_apprx_tanh
 
 P = 128
 S = E * C
-HALF = 512
 PAIR = 2 * C
 
 XCUT = 768
 I1 = [[["S", 0, 128]]] * E
 I3 = [[["V", 0, 128]] if e in (0, 1, 2, 4, 6) else [["S", 0, 128]] for e in range(E)]
+I2 = [[["V", 0, 256]]] * E
 SC_AFTER = [3, 5, 7, 7]
 LAST = E // 2 - 1
-BUFS = {"raw": 9, "rawx": 2, "raw2": 2, "grp": 4, "grp2": 2, "cod": 3, "cod2": 2, "act": 3}
+BUFS = {"raw": 9, "rawx": 2, "grp": 4, "grp2": 2, "cod": 3, "cod2": 4, "act": 3}
 
 
 def tile_routed_moe_kernel(tc, xT, w1, w3, w2, gate, offs, out):
@@ -41,7 +41,6 @@ def tile_routed_moe_kernel(tc, xT, w1, w3, w2, gate, offs, out):
         keep = ctx.enter_context(tc.tile_pool(name="keep", bufs=1))
         raw = ctx.enter_context(tc.tile_pool(name="raw", bufs=BUFS["raw"]))
         rawx = ctx.enter_context(tc.tile_pool(name="rawx", bufs=BUFS["rawx"]))
-        raw2 = ctx.enter_context(tc.tile_pool(name="raw2", bufs=BUFS["raw2"]))
         grp = ctx.enter_context(tc.tile_pool(name="grp", bufs=BUFS["grp"]))
         grp2 = ctx.enter_context(tc.tile_pool(name="grp2", bufs=BUFS["grp2"]))
         cod = ctx.enter_context(tc.tile_pool(name="cod", bufs=BUFS["cod"]))
@@ -66,7 +65,7 @@ def tile_routed_moe_kernel(tc, xT, w1, w3, w2, gate, offs, out):
 
         xv = xT.rearrange("(p t) n -> p t n", t=4)
         pair = [keep.tile([P, 2 * T], BF16, name="pair%d" % u) for u in range(2)]
-        xg = [keep.tile([P, 4 * HALF], BF16, name="xg%d" % s, align_bytes=64) for s in range(2)]
+        xg = keep.tile([P, 4 * S], BF16, name="xg", align_bytes=64)
         xc = keep.tile([P, S], U32, name="xc", align_bytes=64)
         xs = keep.tile([P, S], U8, name="xs", align_bytes=64)
         rx = []
@@ -80,17 +79,11 @@ def tile_routed_moe_kernel(tc, xT, w1, w3, w2, gate, offs, out):
                     pair[u][:, 2 * n0 : 2 * n1].rearrange("p (n j) -> p n j", j=2),
                     rx[u][:, :, n0:n1].rearrange("p j n -> p n j"),
                 )
-            for s in range(2):
-                nc.vector.tensor_copy(
-                    out=xg[s][:].bitcast(U32).rearrange("p (n u) -> p n u", u=2)[:, :, u],
-                    in_=pair[u][:].bitcast(U32).indirect(offs_sb[:, s * (HALF // 16) : (s + 1) * (HALF // 16)]),
-                )
-        for s in range(2):
-            nc.vector.quantize_mx(
-                out=xc[:, s * HALF : (s + 1) * HALF].bitcast(FP8X4),
-                scales=xs[:, s * HALF : (s + 1) * HALF],
-                in_=xg[s][:],
+            nc.vector.tensor_copy(
+                out=xg[:].bitcast(U32).rearrange("p (n u) -> p n u", u=2)[:, :, u],
+                in_=pair[u][:].bitcast(U32).indirect(offs_sb[:]),
             )
+        nc.vector.quantize_mx(out=xc[:].bitcast(FP8X4), scales=xs[:], in_=xg[:])
 
         w1v = w1.rearrange("e (p j) c -> e p j c", j=4)
         w3v = w3.rearrange("e (p j) c -> e p j c", j=4)
@@ -107,15 +100,17 @@ def tile_routed_moe_kernel(tc, xT, w1, w3, w2, gate, offs, out):
             gate_sb[q] = keep.tile([P, 2, PAIR], F32, name="gate%d" % q)
             nc.sync.dma_start(gate_sb[q][:], gv[:, :, q * PAIR : (q + 1) * PAIR])
 
-        def prep_w2(q, r2):
-            g2 = grp2.tile([P, 8 * N], BF16, name="g2", align_bytes=64)
-            nc.vector.tensor_copy(
-                out=g2[:].rearrange("p (l c i j) -> p l c j i", l=2, i=4, j=4),
-                in_=r2[:].rearrange("p l (j c i) -> p l c j i", j=4, i=4),
-            )
-            wc2[q] = cod2.tile([P, 2 * N], U32, name="wc2", align_bytes=64)
-            ws2[q] = cod2.tile([P, 2 * N], U8, name="ws2", align_bytes=64)
-            nc.vector.quantize_mx(out=wc2[q][:].bitcast(FP8X4), scales=ws2[q][:], in_=g2[:])
+        def prep_w2(e, r2):
+            g2 = grp2.tile([P, 4 * N], BF16, name="g2", align_bytes=64)
+            for eng, c0, c1 in I2[e]:
+                copy_on(
+                    eng,
+                    g2[:, 4 * c0 : 4 * c1].rearrange("p (c i j) -> p c j i", i=4, j=4),
+                    r2.rearrange("p (j c) -> p j c", j=4)[:, :, c0:c1].rearrange("p j (c i) -> p c j i", i=4),
+                )
+            wc2[e] = cod2.tile([P, N], U32, name="wc2", align_bytes=64)
+            ws2[e] = cod2.tile([P, N], U8, name="ws2", align_bytes=64)
+            nc.vector.quantize_mx(out=wc2[e][:].bitcast(FP8X4), scales=ws2[e][:], in_=g2[:])
 
         def scatter(q):
             cols = offs_sb[:, q * (PAIR // 16) : (q + 1) * (PAIR // 16)]
@@ -134,23 +129,39 @@ def tile_routed_moe_kernel(tc, xT, w1, w3, w2, gate, offs, out):
                 nc.sync.dma_start(r[:], wv[e])
                 raws.append(r)
             if el == 1:
-                r2 = raw2.tile([P, 2, 4 * N], F32, name="rw2")
+                r2 = rawx.tile([P, 2, 4 * N], F32, name="rwx")
                 nc.sync.dma_start(r2[:], w2v[q])
                 if q == LAST:
                     load_gate(q)
             elif q > 0:
                 load_gate(q - 1)
-            for which, r, parts, pool in (("1", raws[0], I1[e], ps_a), ("3", raws[1], I3[e], ps_b)):
-                g = grp.tile([P, 4 * H], BF16, name="g13", align_bytes=64)
+            joint = e == 0
+            if joint:
+                g0 = keep.tile([P, 8 * H], BF16, name="g0", align_bytes=64)
+                wc0 = keep.tile([P, 2 * H], U32, name="wc0", align_bytes=64)
+                ws0 = keep.tile([P, 2 * H], U8, name="ws0", align_bytes=64)
+            prepared = []
+            for k, (which, r, parts) in enumerate((("1", raws[0], I1[e]), ("3", raws[1], I3[e]))):
+                if joint:
+                    g = g0[:, k * 4 * H : (k + 1) * 4 * H]
+                    wc, ws = wc0[:, k * H : (k + 1) * H], ws0[:, k * H : (k + 1) * H]
+                else:
+                    gt = grp.tile([P, 4 * H], BF16, name="g13", align_bytes=64)
+                    wct = cod.tile([P, H], U32, name="wc" + which, align_bytes=64)
+                    wst = cod.tile([P, H], U8, name="ws" + which, align_bytes=64)
+                    g, wc, ws = gt[:], wct[:], wst[:]
                 for eng, m0, m1 in parts:
                     copy_on(
                         eng,
-                        g[:].rearrange("p (t m j) -> p m j t", t=4, j=4)[:, m0:m1],
+                        g.rearrange("p (t m j) -> p m j t", t=4, j=4)[:, m0:m1],
                         r[:].rearrange("p j (m t) -> p m j t", t=4)[:, m0:m1],
                     )
-                wc = cod.tile([P, H], U32, name="wc" + which, align_bytes=64)
-                ws = cod.tile([P, H], U8, name="ws" + which, align_bytes=64)
-                nc.vector.quantize_mx(out=wc[:].bitcast(FP8X4), scales=ws[:], in_=g[:])
+                if not joint:
+                    nc.vector.quantize_mx(out=wc.bitcast(FP8X4), scales=ws, in_=g)
+                prepared.append((which, wc, ws))
+            if joint:
+                nc.vector.quantize_mx(out=wc0[:].bitcast(FP8X4), scales=ws0[:], in_=g0[:])
+            for (which, wc, ws), pool in zip(prepared, (ps_a, ps_b)):
                 bank = pool.tile([P, 4, C], F32, name="bank" + which)
                 for t in range(4):
                     nc.tensor.matmul_mx(
@@ -184,7 +195,8 @@ def tile_routed_moe_kernel(tc, xT, w1, w3, w2, gate, offs, out):
                 op=MULT,
             )
             if el == 1:
-                prep_w2(q, r2)
+                for l in range(2):
+                    prep_w2(2 * q + l, r2[:, l, :])
             if q == LAST:
                 nc.vector.quantize_mx(
                     out=hc[:, el * C : (el + 1) * C].bitcast(FP8X4),
@@ -205,11 +217,11 @@ def tile_routed_moe_kernel(tc, xT, w1, w3, w2, gate, offs, out):
                     pys = [py[:, 0, :], py[:, 1, :]]
                 for nt in range(2):
                     for l in range(2):
-                        w0 = l * N + nt * P
+                        ee = 2 * q + l
                         nc.tensor.matmul_mx(
                             out=pys[nt][:, l * C : (l + 1) * C],
-                            lhsT=wc2[q][:, w0 : w0 + P].bitcast(FP8X4),
-                            lhsT_scale=ws2[q][:, w0 : w0 + P],
+                            lhsT=wc2[ee][:, nt * P : (nt + 1) * P].bitcast(FP8X4),
+                            lhsT_scale=ws2[ee][:, nt * P : (nt + 1) * P],
                             rhs=hc[:, l * C : (l + 1) * C].bitcast(FP8X4),
                             rhs_scale=hs[:, l * C : (l + 1) * C],
                             start=True,

@@ -153,8 +153,8 @@ def tile_routed_moe_kernel(tc, xT, w1, w3, w2, gate, offs, out):
                 for eng, m0, m1 in parts:
                     copy_on(
                         eng,
-                        g.rearrange("p (t m j) -> p m j t", t=4, j=4)[:, m0:m1],
-                        r[:].rearrange("p j (m t) -> p m j t", t=4)[:, m0:m1],
+                        g.rearrange("p (h l m j) -> p h m j l", h=2, l=2, j=4)[:, :, m0:m1],
+                        r[:].rearrange("p j (m h l) -> p h m j l", h=2, l=2)[:, :, m0:m1],
                     )
                 if not joint:
                     nc.vector.quantize_mx(out=wc.bitcast(FP8X4), scales=ws, in_=g)

@@ -19,11 +19,12 @@ S = E * C
 PAIR = 2 * C
 
 XCUT = 768
-I1 = [[["S", 0, 128]]] * E
-I3 = [[["V", 0, 128]] if e in (0, 1, 2, 4, 6) else [["S", 0, 128]] for e in range(E)]
+I1 = [[["V", 0, 128]] if e == E - 1 else [["S", 0, 128]] for e in range(E)]
+I3 = [[["V", 0, 128]] if e in (0, 1, 2, 4) else [["S", 0, 128]] for e in range(E)]
 I2 = [[["V", 0, 256]]] * E
 SC_AFTER = [3, 5, 7, 7]
 LAST = E // 2 - 1
+YSPLIT = (LAST - 1, LAST)
 BUFS = {"raw": 9, "rawx": 2, "grp": 4, "grp2": 2, "cod": 3, "cod2": 4, "act": 3}
 
 
@@ -207,7 +208,7 @@ def tile_routed_moe_kernel(tc, xT, w1, w3, w2, gate, offs, out):
                 if q != LAST:
                     nc.vector.quantize_mx(out=hc[:].bitcast(FP8X4), scales=hs[:], in_=hb[:])
                 ysb[q] = ysp.tile([P, 2, PAIR], F32, name="ysb")
-                if q == LAST:
+                if q in YSPLIT:
                     pys = []
                     for nt in range(2):
                         py = ps_y.tile([P, PAIR], F32, name="py")
@@ -227,9 +228,9 @@ def tile_routed_moe_kernel(tc, xT, w1, w3, w2, gate, offs, out):
                             start=True,
                             stop=True,
                         )
-                    if q == LAST:
+                    if q in YSPLIT:
                         nc.scalar.copy(out=ysb[q][:, nt, :], in_=pys[nt])
-                if q != LAST:
+                if q not in YSPLIT:
                     nc.scalar.copy(out=ysb[q][:], in_=py[:])
             for qq in range(E // 2):
                 if SC_AFTER[qq] == e:

@@ -20,7 +20,7 @@ PAIR = 2 * C
 
 XCUT = 768
 I1 = [[["V", 0, 128]] if e == E - 1 else [["S", 0, 128]] for e in range(E)]
-I3 = [[["V", 0, 128]] if e in (0, 1, 2, 4) else [["S", 0, 128]] for e in range(E)]
+I3 = [[["V", 0, 128]] if e in (0, 2, 4) else [["S", 0, 128]] for e in range(E)]
 I2 = [[["V", 0, 256]]] * E
 SC_AFTER = [3, 5, 7, 7]
 LAST = E // 2 - 1
@@ -132,11 +132,8 @@ def tile_routed_moe_kernel(tc, xT, w1, w3, w2, gate, offs, out):
             if el == 1:
                 r2 = rawx.tile([P, 2, 4 * N], F32, name="rwx")
                 nc.sync.dma_start(r2[:], w2v[q])
-                if q == LAST:
-                    load_gate(q)
-            elif q > 0:
-                load_gate(q - 1)
-            joint = e == 0
+                load_gate(q)
+            joint = False
             if joint:
                 g0 = keep.tile([P, 8 * H], BF16, name="g0", align_bytes=64)
                 wc0 = keep.tile([P, 2 * H], U32, name="wc0", align_bytes=64)

@@ -24,7 +24,7 @@ I3 = [[["V", 0, 128]] if e in (0, 2, 4) else [["S", 0, 128]] for e in range(E)]
 I2 = [[["V", 0, 256]]] * E
 SC_AFTER = [3, 5, 7, 7]
 LAST = E // 2 - 1
-YSPLIT = (LAST - 1, LAST)
+YSPLIT = range(E // 2)
 BUFS = {"raw": 9, "rawx": 2, "grp": 4, "grp2": 2, "cod": 3, "cod2": 4, "act": 3}
 
 

from contextlib import ExitStack

import concourse.mybir as mybir

K, T, E, C, H, N = 512, 2048, 8, 128, 512, 256
FLOPS = 2 * E * C * (2 * K * H + H * N)

F32 = mybir.dt.float32
BF16 = mybir.dt.bfloat16
U32 = mybir.dt.uint32
U16 = mybir.dt.uint16
U8 = mybir.dt.uint8
FP8X4 = mybir.dt.float8_e4m3fn_x4
MULT = mybir.AluOpType.mult
GELU = mybir.ActivationFunctionType.Gelu_apprx_tanh

P = 128
S = E * C
PAIR = 2 * C

XCUT = 768
I1 = [[["V", 0, 128]] if e == E - 1 else [["S", 0, 128]] for e in range(E)]
I3 = [[["V", 0, 128]] if e in (0, 2, 4) else [["S", 0, 128]] for e in range(E)]
I2 = [[["V", 0, 256]]] * E
SC_AFTER = [3, 5, 7, 7]
LAST = E // 2 - 1
YSPLIT = range(E // 2)
BUFS = {"raw": 9, "rawx": 2, "grp": 4, "grp2": 2, "cod": 3, "cod2": 4, "act": 3}


def tile_routed_moe_kernel(tc, xT, w1, w3, w2, gate, offs, out):
    nc = tc.nc

    def copy_on(eng, dst, src):
        if eng == "S":
            nc.scalar.copy(out=dst, in_=src)
        else:
            nc.vector.tensor_copy(out=dst, in_=src)

    with ExitStack() as ctx:
        lists = ctx.enter_context(tc.tile_pool(name="lists", bufs=1))
        keep = ctx.enter_context(tc.tile_pool(name="keep", bufs=1))
        raw = ctx.enter_context(tc.tile_pool(name="raw", bufs=BUFS["raw"]))
        rawx = ctx.enter_context(tc.tile_pool(name="rawx", bufs=BUFS["rawx"]))
        grp = ctx.enter_context(tc.tile_pool(name="grp", bufs=BUFS["grp"]))
        grp2 = ctx.enter_context(tc.tile_pool(name="grp2", bufs=BUFS["grp2"]))
        cod = ctx.enter_context(tc.tile_pool(name="cod", bufs=BUFS["cod"]))
        cod2 = ctx.enter_context(tc.tile_pool(name="cod2", bufs=BUFS["cod2"]))
        act = ctx.enter_context(tc.tile_pool(name="act", bufs=BUFS["act"]))
        ysp = ctx.enter_context(tc.tile_pool(name="ysp", bufs=4))
        hid = ctx.enter_context(tc.tile_pool(name="hid", bufs=2))
        ps_a = ctx.enter_context(tc.psum_pool(name="ps_a", bufs=3))
        ps_b = ctx.enter_context(tc.psum_pool(name="ps_b", bufs=3))
        ps_y = ctx.enter_context(tc.psum_pool(name="ps_y", bufs=2))

        offs_sb = lists.tile([P, S // 16], U16, name="offs_sb")
        nc.sync.dma_start(offs_sb[:], offs)

        warm = keep.tile([P, 1], F32, name="warm")
        nc.vector.memset(warm[:], 0.0)
        nc.scalar.activation(out=warm[:], in_=warm[:], func=GELU)

        win = [keep.tile([P, T], F32, name="win%d" % nt) for nt in range(2)]
        for nt in range(2):
            nc.vector.memset(win[nt][:], 0.0)

        xv = xT.rearrange("(p t) n -> p t n", t=4)
        pair = [keep.tile([P, 2 * T], BF16, name="pair%d" % u) for u in range(2)]
        xg = keep.tile([P, 4 * S], BF16, name="xg", align_bytes=64)
        xc = keep.tile([P, S], U32, name="xc", align_bytes=64)
        xs = keep.tile([P, S], U8, name="xs", align_bytes=64)
        rx = []
        for u in range(2):
            rx.append(rawx.tile([P, 2, T], F32, name="rwx"))
            nc.sync.dma_start(rx[u][:], xv[:, 2 * u : 2 * u + 2, :])
        for u in range(2):
            for eng, n0, n1 in (("S", 0, XCUT), ("V", XCUT, T)):
                copy_on(
                    eng,
                    pair[u][:, 2 * n0 : 2 * n1].rearrange("p (n j) -> p n j", j=2),
                    rx[u][:, :, n0:n1].rearrange("p j n -> p n j"),
                )
            nc.vector.tensor_copy(
                out=xg[:].bitcast(U32).rearrange("p (n u) -> p n u", u=2)[:, :, u],
                in_=pair[u][:].bitcast(U32).indirect(offs_sb[:]),
            )
        nc.vector.quantize_mx(out=xc[:].bitcast(FP8X4), scales=xs[:], in_=xg[:])

        w1v = w1.rearrange("e (p j) c -> e p j c", j=4)
        w3v = w3.rearrange("e (p j) c -> e p j c", j=4)
        w2v = w2.rearrange("(q e) (p j) c -> q p e (j c)", e=2, j=4)
        gv = gate.rearrange("(nt p) s -> p nt s", p=P)

        gate_sb = {}
        wc2 = {}
        ws2 = {}
        ysb = {}
        state = {}

        def load_gate(q):
            gate_sb[q] = keep.tile([P, 2, PAIR], F32, name="gate%d" % q)
            nc.sync.dma_start(gate_sb[q][:], gv[:, :, q * PAIR : (q + 1) * PAIR])

        def prep_w2(e, r2):
            g2 = grp2.tile([P, 4 * N], BF16, name="g2", align_bytes=64)
            for eng, c0, c1 in I2[e]:
                copy_on(
                    eng,
                    g2[:, 4 * c0 : 4 * c1].rearrange("p (c i j) -> p c j i", i=4, j=4),
                    r2.rearrange("p (j c) -> p j c", j=4)[:, :, c0:c1].rearrange("p j (c i) -> p c j i", i=4),
                )
            wc2[e] = cod2.tile([P, N], U32, name="wc2", align_bytes=64)
            ws2[e] = cod2.tile([P, N], U8, name="ws2", align_bytes=64)
            nc.vector.quantize_mx(out=wc2[e][:].bitcast(FP8X4), scales=ws2[e][:], in_=g2[:])

        def scatter(q):
            cols = offs_sb[:, q * (PAIR // 16) : (q + 1) * (PAIR // 16)]
            for nt in range(2):
                nc.vector.tensor_tensor(
                    out=win[nt][:].indirect(cols), in0=ysb[q][:, nt, :], in1=gate_sb[q][:, nt, :], op=MULT
                )

        for e in range(E):
            el = e % 2
            q = e // 2
            banks = []
            raws = []
            for wv in (w1v, w3v):
                r = raw.tile([P, 4, H], F32, name="rw")
                nc.sync.dma_start(r[:], wv[e])
                raws.append(r)
            if el == 1:
                r2 = rawx.tile([P, 2, 4 * N], F32, name="rwx")
                nc.sync.dma_start(r2[:], w2v[q])
                load_gate(q)
            joint = False
            if joint:
                g0 = keep.tile([P, 8 * H], BF16, name="g0", align_bytes=64)
                wc0 = keep.tile([P, 2 * H], U32, name="wc0", align_bytes=64)
                ws0 = keep.tile([P, 2 * H], U8, name="ws0", align_bytes=64)
            prepared = []
            for k, (which, r, parts) in enumerate((("1", raws[0], I1[e]), ("3", raws[1], I3[e]))):
                if joint:
                    g = g0[:, k * 4 * H : (k + 1) * 4 * H]
                    wc, ws = wc0[:, k * H : (k + 1) * H], ws0[:, k * H : (k + 1) * H]
                else:
                    gt = grp.tile([P, 4 * H], BF16, name="g13", align_bytes=64)
                    wct = cod.tile([P, H], U32, name="wc" + which, align_bytes=64)
                    wst = cod.tile([P, H], U8, name="ws" + which, align_bytes=64)
                    g, wc, ws = gt[:], wct[:], wst[:]
                for eng, m0, m1 in parts:
                    copy_on(
                        eng,
                        g.rearrange("p (h l m j) -> p h m j l", h=2, l=2, j=4)[:, :, m0:m1],
                        r[:].rearrange("p j (m h l) -> p h m j l", h=2, l=2)[:, :, m0:m1],
                    )
                if not joint:
                    nc.vector.quantize_mx(out=wc.bitcast(FP8X4), scales=ws, in_=g)
                prepared.append((which, wc, ws))
            if joint:
                nc.vector.quantize_mx(out=wc0[:].bitcast(FP8X4), scales=ws0[:], in_=g0[:])
            for (which, wc, ws), pool in zip(prepared, (ps_a, ps_b)):
                bank = pool.tile([P, 4, C], F32, name="bank" + which)
                for t in range(4):
                    nc.tensor.matmul_mx(
                        out=bank[:, t, :],
                        lhsT=wc[:, t * P : (t + 1) * P].bitcast(FP8X4),
                        lhsT_scale=ws[:, t * P : (t + 1) * P],
                        rhs=xc[:, e * C : (e + 1) * C].bitcast(FP8X4),
                        rhs_scale=xs[:, e * C : (e + 1) * C],
                        start=True,
                        stop=True,
                    )
                banks.append(bank)

            gl = act.tile([P, 4 * C], F32, name="gl")
            nc.scalar.activation(
                out=gl[:].rearrange("p (n t) -> p n t", t=4),
                in_=banks[0][:].rearrange("p t n -> p n t"),
                func=GELU,
            )
            if el == 0:
                state["hb"] = hid.tile([P, 4 * PAIR], BF16, name="hb", align_bytes=64)
                state["hc"] = hid.tile([P, PAIR], U32, name="hc", align_bytes=64)
                state["hs"] = hid.tile([P, PAIR], U8, name="hs", align_bytes=64)
            hb = state["hb"]
            hc = state["hc"]
            hs = state["hs"]
            nc.vector.tensor_tensor(
                out=hb[:, el * 4 * C : (el + 1) * 4 * C].rearrange("p (n t) -> p n t", t=4),
                in0=gl[:].rearrange("p (n t) -> p n t", t=4),
                in1=banks[1][:].rearrange("p t n -> p n t"),
                op=MULT,
            )
            if el == 1:
                for l in range(2):
                    prep_w2(2 * q + l, r2[:, l, :])
            if q == LAST:
                nc.vector.quantize_mx(
                    out=hc[:, el * C : (el + 1) * C].bitcast(FP8X4),
                    scales=hs[:, el * C : (el + 1) * C],
                    in_=hb[:, el * 4 * C : (el + 1) * 4 * C],
                )
            if el == 1:
                if q != LAST:
                    nc.vector.quantize_mx(out=hc[:].bitcast(FP8X4), scales=hs[:], in_=hb[:])
                ysb[q] = ysp.tile([P, 2, PAIR], F32, name="ysb")
                if q in YSPLIT:
                    pys = []
                    for nt in range(2):
                        py = ps_y.tile([P, PAIR], F32, name="py")
                        pys.append(py[:])
                else:
                    py = ps_y.tile([P, 2, PAIR], F32, name="py")
                    pys = [py[:, 0, :], py[:, 1, :]]
                for nt in range(2):
                    for l in range(2):
                        ee = 2 * q + l
                        nc.tensor.matmul_mx(
                            out=pys[nt][:, l * C : (l + 1) * C],
                            lhsT=wc2[ee][:, nt * P : (nt + 1) * P].bitcast(FP8X4),
                            lhsT_scale=ws2[ee][:, nt * P : (nt + 1) * P],
                            rhs=hc[:, l * C : (l + 1) * C].bitcast(FP8X4),
                            rhs_scale=hs[:, l * C : (l + 1) * C],
                            start=True,
                            stop=True,
                        )
                    if q in YSPLIT:
                        nc.scalar.copy(out=ysb[q][:, nt, :], in_=pys[nt])
                if q not in YSPLIT:
                    nc.scalar.copy(out=ysb[q][:], in_=py[:])
            for qq in range(E // 2):
                if SC_AFTER[qq] == e:
                    scatter(qq)
        for nt in range(2):
            nc.sync.dma_start(out[nt * P : (nt + 1) * P, :], win[nt][:])
